import numpy as np
import ml_dtypes


def mxq(x, axis, fmt="e4m3"):
    dtype, down = {"e4m3": (ml_dtypes.float8_e4m3fn, 7), "e5m2": (ml_dtypes.float8_e5m2, 14)}[fmt]
    v = np.moveaxis(np.asarray(x, np.float32).astype(ml_dtypes.bfloat16).astype(np.float64), axis, -1)
    blocks = v.reshape(v.shape[:-1] + (-1, 32))
    amax = np.abs(blocks).max(-1, keepdims=True)
    byte = np.maximum(np.where(amax > 0, np.frexp(amax)[1] - 1 + 127, 0) - down, 1)
    scale = np.exp2(byte - 127.0)
    codes = (blocks / scale).astype(np.float32).astype(dtype).astype(np.float64)
    return np.moveaxis((codes * scale).reshape(v.shape), -1, axis)


WIDE = False


def mx_kscale(k):
    if not WIDE:
        return np.ones(k)
    levels = np.array([10, -10, 5, -5, 0])
    if k % 512:
        return np.exp2(np.random.permutation(np.resize(levels, k // 32))).repeat(32)
    a = np.empty((k // 512, 16))
    for p in range(k // 512):
        a[p, :8] = np.random.permutation(np.resize(levels, 8))
        for g in range(8):
            far = levels[np.abs(levels - a[p, g]) >= 10]
            a[p, g + 8] = far[np.random.randint(len(far))]
    return np.exp2(a.ravel()).repeat(32)


def f64(x):
    return np.asarray(x).astype(np.float64)


def striped(idx):
    return np.tile(np.asarray(idx).reshape(-1, 16).T, (8, 1)).astype(np.uint16)


def unstriped(offs):
    return offs[:16].T.reshape(-1).astype(np.int64)


E2M1 = np.array([0.0, 0.5, 1.0, 1.5, 2.0, 3.0, 4.0, 6.0, -0.0, -0.5, -1.0, -1.5, -2.0, -3.0, -4.0, -6.0])


def pack_weight(w, fmt):
    k, n = w.shape
    w = f64(np.asarray(w, np.float32).astype(ml_dtypes.bfloat16)).reshape(k // 32, 32, n)
    amax = np.abs(w).max(1)
    if fmt == "e4m3":
        byte = np.frexp(amax)[1] - 1 + 127 - 7
    else:
        mant, ex = np.frexp(amax / 6.0)
        byte = np.where(mant > 0.5, ex, ex - 1) + 127
    byte = np.clip(np.where(amax > 0, byte, 1), 1, 254)
    scaled = (w * np.exp2(127.0 - byte)[:, None, :]).reshape(k, n).astype(np.float32)
    by_word = np.ascontiguousarray(scaled.reshape(k // 512, 128, 4, n).transpose(0, 1, 3, 2))
    if fmt == "e4m3":
        words = by_word.astype(ml_dtypes.float8_e4m3fn).view(np.uint8)
    else:
        c = by_word.astype(ml_dtypes.float4_e2m1fn).view(np.uint8) & 0xF
        words = (c[..., 0::2] | (c[..., 1::2] << 4)).reshape(k // 512, 128, 2 * n)
    return np.ascontiguousarray(words), np.ascontiguousarray(byte.astype(np.uint8).reshape(k // 512, 16, n))


def unpack_weight(words, scales, fmt):
    g, _, n = scales.shape
    words = np.ascontiguousarray(words).reshape(g, 128, n, -1)
    if fmt == "e4m3":
        vals = words.view(ml_dtypes.float8_e4m3fn).astype(np.float64)
    else:
        nib = np.empty((g, 128, n, 4), np.uint8)
        nib[..., 0::2] = words & 0xF
        nib[..., 1::2] = words >> 4
        vals = E2M1[nib]
    vals = vals * np.repeat(np.exp2(scales.astype(np.float64) - 127.0), 8, axis=1)[..., None]
    return vals.transpose(0, 1, 3, 2).reshape(g * 512, n)


B, N, T, D, DV, NQ = 1, 1536, 4096, 512, 256, 128
PAGE = 512


def setup_inputs():
    n = np.random.standard_normal
    pages = np.random.permutation(T // PAGE)[:B * N // PAGE]
    idx = (pages[:, None] * PAGE + np.arange(PAGE)[None, :]).reshape(-1)
    s = mx_kscale(D)[:, None]
    u = np.ones(T)
    u[idx] = mx_kscale(B * N)
    r = np.random.uniform(0.5, 2.0, T)
    k = n((D, T)) / s
    v = n((DV, T)) / (u * r)
    kp = pack_weight(k, "e4m3")
    vp = pack_weight(v.T, "e4m3")
    return {
        "qT": (n((B, D, NQ)) * s * (1.00 / np.sqrt(D))).astype(np.float32),
        "k_words": kp[0],
        "k_scales": kp[1],
        "v_words": vp[0],
        "v_scales": vp[1],
        "vs": np.tile(u * r, (128, 1)).astype(np.float32),
        "kb": np.tile(n(T), (128, 1)).astype(np.float32),
        "offs": striped(idx),
        "voffs": striped((pages[:, None] * DV + np.arange(DV)[None, :]).reshape(-1)),
    }


def reference(qT, k_words, k_scales, v_words, v_scales, vs, kb, offs, voffs):
    idx = unstriped(offs)
    k = unpack_weight(k_words, k_scales, "e4m3")
    v = unpack_weight(v_words, v_scales, "e4m3")
    v = v.reshape(T // 512, 512, DV)[unstriped(voffs)[::DV] // DV].reshape(B, N, DV)
    pick = lambda x: x[:, idx].reshape(x.shape[0], B, N).transpose(1, 0, 2)
    q = f64(qT)
    score = mxq(q, 1, "e4m3").transpose(0, 2, 1) @ pick(k)
    score = score + pick(f64(kb))[:, :1, :]
    p = score / (1.0 + np.exp(-score))
    w = p * pick(f64(vs))[:, :1, :]
    y = mxq(w, 2, "e4m3") @ v
    y = y / 16.0
    return y

@@ -1,0 +1,154 @@
+from contextlib import ExitStack
+
+import concourse.mybir as mybir
+from concourse.masks import make_identity
+
+N, T, D, DV, NQ = 1536, 4096, 512, 256, 128
+P = 128
+PACK = 4
+PAGE = 512
+PAGES = N // PAGE
+POOL_PAGES = T // PAGE
+BYTES = 4 * D * NQ + T * (D + DV) + T * (D + DV) // 32 + 2 * 4 * T + 2 * P * (N + PAGES * DV) // 16 + 4 * NQ * DV
+FLOPS = 2 * NQ * N * (D + DV)
+
+F32 = mybir.dt.float32
+BF16 = mybir.dt.bfloat16
+I32 = mybir.dt.int32
+U32 = mybir.dt.uint32
+U16 = mybir.dt.uint16
+U8 = mybir.dt.uint8
+FP8X4 = mybir.dt.float8_e4m3fn_x4
+ACT = mybir.ActivationFunctionType
+
+
+def tile_attend_pkv8_silu_bias_kernel(tc, qT, k_words, k_scales, v_words, v_scales, vs, kb, offs, voffs, out):
+    nc = tc.nc
+    with ExitStack() as ctx:
+        keep = ctx.enter_context(tc.tile_pool(name="keep", bufs=1))
+        psum = ctx.enter_context(tc.psum_pool(name="psum", bufs=1))
+
+        slots = keep.tile([P, N // 16], U16, name="slots")
+        vcols = keep.tile([P, PAGES * DV // 16], U16, name="vcols")
+        ks_pool = keep.tile([P, T], U8, name="ks_pool", tag="b", align_bytes=64)
+        kb_pool = keep.tile([P, T], F32, name="kb_pool", tag="c", align_bytes=64)
+        q_raw = keep.tile([P, PACK, NQ], F32, name="q_raw", tag="a", align_bytes=64)
+        ident = keep.tile([P, P], F32, name="ident", align_bytes=64)
+
+        nc.vector.memset(ks_pool[:].bitcast(I32), 0)
+        nc.vector.memset(kb_pool[:].bitcast(I32), 0)
+        make_identity(nc, ident[:])
+        warm = keep.tile([P, 1], F32, name="warm")
+        nc.scalar.activation(warm[:], ident[:, 0:1], ACT.Silu)
+
+        nc.sync.dma_start(slots[:], offs)
+        ks_rows = k_scales[0].rearrange("(a r) c -> r a c", r=PACK)
+        for r in range(PACK):
+            nc.sync.dma_start(ks_pool[r:P:32, :].bitcast(I32), ks_rows[r].bitcast(I32))
+        nc.sync.dma_start(q_raw[:], qT[0].rearrange("(p j) q -> p j q", j=PACK))
+        nc.scalar.dma_start(kb_pool[0:1, :], kb[0:1, :])
+        nc.sync.dma_start(vcols[:], voffs)
+
+        def page_slots(g):
+            return slots[:, g * (PAGE // 16) : (g + 1) * (PAGE // 16)]
+
+        ks = keep.tile([P, N], U8, name="ks", align_bytes=64)
+        nc.vector.tensor_copy(ks[:], ks_pool[:].indirect(slots[:]))
+
+        q_bf = keep.tile([P, NQ, PACK], BF16, name="q_bf", align_bytes=64)
+        nc.scalar.copy(q_bf[:], q_raw[:].rearrange("p j q -> p q j"))
+        kw_pool = keep.tile([P, T], U32, name="kw_pool", tag="a", align_bytes=64)
+        nc.sync.dma_start(kw_pool[:].bitcast(I32), k_words[0].rearrange("p n r -> p (n r)").bitcast(I32))
+        vs_pool = keep.tile([P, T], F32, name="vs_pool", tag="b", align_bytes=64)
+        nc.sync.dma_start(vs_pool[:], vs)
+        q_codes = keep.tile([P, NQ], U32, name="q_codes", align_bytes=64)
+        q_scales = keep.tile([P, NQ], U8, name="q_scales", align_bytes=64)
+        nc.vector.quantize_mx(q_codes[:].bitcast(FP8X4), q_scales[:], q_bf[:].rearrange("p q j -> p (q j)"))
+
+        kb_row = keep.tile([P, N], F32, name="kb_row", align_bytes=64)
+        nc.vector.tensor_copy(kb_row[:], kb_pool[:].indirect(slots[:]))
+
+        vw_pool = keep.tile([P, POOL_PAGES * DV], U32, name="vw_pool", tag="c", align_bytes=64)
+        nc.sync.dma_start(
+            vw_pool[:].bitcast(I32).rearrange("p (u e) -> p u e", u=POOL_PAGES),
+            v_words.rearrange("u p e r -> p u (e r)").bitcast(I32),
+        )
+
+        def to_columns(row, name):
+            bank = psum.tile([P, PACK, P], F32, name=name + "_bank", tag="turn", bufs=3)
+            for t in range(PACK):
+                nc.tensor.transpose(bank[:, t, :], row[:, t:PAGE:PACK], ident[:])
+            col = keep.tile([P, PACK], F32, name=name)
+            nc.scalar.copy(col[:], bank[:, :, 0])
+            return col
+
+        kb_col = [to_columns(kb_row[:, g * PAGE : (g + 1) * PAGE], "kb_col%d" % g) for g in range(PAGES)]
+
+        silu = []
+        for g in range(PAGES):
+            kw = keep.tile([P, PAGE], U32, name="kw%d" % g, align_bytes=64)
+            nc.vector.tensor_copy(kw[:], kw_pool[:].indirect(page_slots(g)))
+            score = psum.tile([P, PAGE], F32, name="score%d" % g, tag="score", bufs=2)
+            nc.tensor.matmul_mx(
+                score[:],
+                lhsT=q_codes[:].bitcast(FP8X4),
+                lhsT_scale=q_scales[:],
+                rhs=kw[:].bitcast(FP8X4),
+                rhs_scale=ks[:, g * PAGE : (g + 1) * PAGE],
+                start=True,
+                stop=True,
+            )
+            dealt = keep.tile([P, PACK, P], F32, name="dealt%d" % g, align_bytes=64)
+            nc.scalar.copy(dealt[:], score[:].rearrange("q (s t) -> q t s", t=PACK))
+            turned = psum.tile([P, PACK, NQ], F32, name="turned%d" % g, tag="turned", bufs=2)
+            for t in range(PACK):
+                nc.tensor.transpose(turned[:, t, :], dealt[:, t, :], ident[:])
+            p = keep.tile([P, PACK, NQ], F32, name="p%d" % g, align_bytes=64)
+            for t in range(PACK):
+                nc.scalar.activation(p[:, t, :], turned[:, t, :], ACT.Silu, bias=kb_col[g][:, t : t + 1])
+            silu.append(p)
+
+        vsc_pool = keep.tile([P, POOL_PAGES * DV], U8, name="vsc_pool", tag="a", align_bytes=64)
+        nc.vector.memset(vsc_pool[:].bitcast(I32), 0)
+        vsc_rows = v_scales.rearrange("u (a r) e -> r a u e", r=PACK)
+        for r in range(PACK):
+            nc.sync.dma_start(
+                vsc_pool[r:P:32, :].bitcast(I32).rearrange("a (u e) -> a u e", u=POOL_PAGES),
+                vsc_rows[r].bitcast(I32),
+            )
+
+        w_codes, w_scales = [], []
+        for g in range(PAGES):
+            vs_row = keep.tile([P, PAGE], F32, name="vs_row%d" % g, align_bytes=64)
+            nc.vector.tensor_copy(vs_row[:], vs_pool[:].indirect(page_slots(g)))
+            vs_col = to_columns(vs_row, "vs_col%d" % g)
+            w = keep.tile([P, PACK, NQ], BF16, name="w%d" % g, align_bytes=64)
+            for t in range(PACK):
+                nc.scalar.activation(w[:, t, :], silu[g][:, t, :], ACT.Copy, scale=vs_col[:, t : t + 1])
+            woven = keep.tile([P, NQ, PACK], BF16, name="woven%d" % g, align_bytes=64)
+            nc.scalar.copy(woven[:], w[:].rearrange("s t q -> s q t"))
+            w_codes.append(keep.tile([P, NQ], U32, name="w_codes%d" % g, align_bytes=64))
+            w_scales.append(keep.tile([P, NQ], U8, name="w_scales%d" % g, align_bytes=64))
+            silu[g] = woven
+
+        vsc = keep.tile([P, PAGES * DV], U8, name="vsc", align_bytes=64)
+        nc.vector.tensor_copy(vsc[:], vsc_pool[:].indirect(vcols[:]))
+        y = psum.tile([P, DV], F32, name="y", tag="y", bufs=1)
+        for g in range(PAGES):
+            vw = keep.tile([P, DV], U32, name="vw%d" % g, align_bytes=64)
+            nc.vector.tensor_copy(vw[:], vw_pool[:].indirect(vcols[:, g * (DV // 16) : (g + 1) * (DV // 16)]))
+            nc.vector.quantize_mx(
+                w_codes[g][:].bitcast(FP8X4), w_scales[g][:], silu[g][:].rearrange("s q t -> s (q t)")
+            )
+            nc.tensor.matmul_mx(
+                y[:],
+                lhsT=w_codes[g][:].bitcast(FP8X4),
+                lhsT_scale=w_scales[g][:],
+                rhs=vw[:].bitcast(FP8X4),
+                rhs_scale=vsc[:, g * DV : (g + 1) * DV],
+                start=(g == 0),
+                stop=(g == PAGES - 1),
+            )
+        result = keep.tile([P, DV], F32, name="result", align_bytes=64)
+        nc.scalar.activation(result[:], y[:], ACT.Copy, scale=1.0 / 16.0)
+        nc.sync.dma_start(out[0], result[:])

@@ -31,22 +31,20 @@ def tile_attend_pkv8_silu_bias_kernel(tc, qT, k_words, k_scales, v_words, v_scal
         slots = keep.tile([P, N // 16], U16, name="slots")
         vcols = keep.tile([P, PAGES * DV // 16], U16, name="vcols")
         ks_pool = keep.tile([P, T], U8, name="ks_pool", tag="b", align_bytes=64)
-        kb_pool = keep.tile([P, T], F32, name="kb_pool", tag="c", align_bytes=64)
+        vs_pool = keep.tile([P, T], F32, name="vs_pool", tag="c", align_bytes=64)
         q_raw = keep.tile([P, PACK, NQ], F32, name="q_raw", tag="a", align_bytes=64)
         ident = keep.tile([P, P], F32, name="ident", align_bytes=64)
 
         nc.vector.memset(ks_pool[:].bitcast(I32), 0)
-        nc.vector.memset(kb_pool[:].bitcast(I32), 0)
+        nc.vector.memset(vs_pool[:].bitcast(I32), 0)
         make_identity(nc, ident[:])
-        warm = keep.tile([P, 1], F32, name="warm")
-        nc.scalar.activation(warm[:], ident[:, 0:1], ACT.Silu)
 
         nc.sync.dma_start(slots[:], offs)
         ks_rows = k_scales[0].rearrange("(a r) c -> r a c", r=PACK)
         for r in range(PACK):
             nc.sync.dma_start(ks_pool[r:P:32, :].bitcast(I32), ks_rows[r].bitcast(I32))
         nc.sync.dma_start(q_raw[:], qT[0].rearrange("(p j) q -> p j q", j=PACK))
-        nc.scalar.dma_start(kb_pool[0:1, :], kb[0:1, :])
+        nc.sync.dma_start(vs_pool[0:1, :], vs[0:1, :])
         nc.sync.dma_start(vcols[:], voffs)
 
         def page_slots(g):
@@ -55,36 +53,30 @@ def tile_attend_pkv8_silu_bias_kernel(tc, qT, k_words, k_scales, v_words, v_scal
         ks = keep.tile([P, N], U8, name="ks", align_bytes=64)
         nc.vector.tensor_copy(ks[:], ks_pool[:].indirect(slots[:]))
 
-        q_bf = keep.tile([P, NQ, PACK], BF16, name="q_bf", align_bytes=64)
+        q_bf = keep.tile([P, NQ, PACK], BF16, name="q_bf", tag="d", align_bytes=64)
         nc.scalar.copy(q_bf[:], q_raw[:].rearrange("p j q -> p q j"))
         kw_pool = keep.tile([P, T], U32, name="kw_pool", tag="a", align_bytes=64)
         nc.sync.dma_start(kw_pool[:].bitcast(I32), k_words[0].rearrange("p n r -> p (n r)").bitcast(I32))
-        vs_pool = keep.tile([P, T], F32, name="vs_pool", tag="b", align_bytes=64)
-        nc.sync.dma_start(vs_pool[:], vs)
-        q_codes = keep.tile([P, NQ], U32, name="q_codes", align_bytes=64)
+        q_codes = keep.tile([P, NQ], U32, name="q_codes", tag="b", align_bytes=64)
         q_scales = keep.tile([P, NQ], U8, name="q_scales", align_bytes=64)
         nc.vector.quantize_mx(q_codes[:].bitcast(FP8X4), q_scales[:], q_bf[:].rearrange("p q j -> p (q j)"))
 
-        kb_row = keep.tile([P, N], F32, name="kb_row", align_bytes=64)
-        nc.vector.tensor_copy(kb_row[:], kb_pool[:].indirect(slots[:]))
-
-        vw_pool = keep.tile([P, POOL_PAGES * DV], U32, name="vw_pool", tag="c", align_bytes=64)
-        nc.sync.dma_start(
-            vw_pool[:].bitcast(I32).rearrange("p (u e) -> p u e", u=POOL_PAGES),
-            v_words.rearrange("u p e r -> p u (e r)").bitcast(I32),
-        )
+        kb_pool = keep.tile([P, T], F32, name="kb_pool", tag="d", align_bytes=64)
+        nc.sync.dma_start(kb_pool[:], kb)
+        vs_row = keep.tile([P, N], F32, name="vs_row", align_bytes=64)
+        nc.vector.tensor_copy(vs_row[:], vs_pool[:].indirect(slots[:]))
 
         def to_columns(row, name):
-            bank = psum.tile([P, PACK, P], F32, name=name + "_bank", tag="turn", bufs=3)
+            bank = psum.tile([P, PACK, P], F32, name=name + "_bank", tag="turn", bufs=2)
             for t in range(PACK):
                 nc.tensor.transpose(bank[:, t, :], row[:, t:PAGE:PACK], ident[:])
             col = keep.tile([P, PACK], F32, name=name)
             nc.scalar.copy(col[:], bank[:, :, 0])
             return col
 
-        kb_col = [to_columns(kb_row[:, g * PAGE : (g + 1) * PAGE], "kb_col%d" % g) for g in range(PAGES)]
+        vs_col = [to_columns(vs_row[:, g * PAGE : (g + 1) * PAGE], "vs_col%d" % g) for g in range(PAGES)]
 
-        silu = []
+        sums = []
         for g in range(PAGES):
             kw = keep.tile([P, PAGE], U32, name="kw%d" % g, align_bytes=64)
             nc.vector.tensor_copy(kw[:], kw_pool[:].indirect(page_slots(g)))
@@ -100,16 +92,19 @@ def tile_attend_pkv8_silu_bias_kernel(tc, qT, k_words, k_scales, v_words, v_scal
             )
             dealt = keep.tile([P, PACK, P], F32, name="dealt%d" % g, align_bytes=64)
             nc.scalar.copy(dealt[:], score[:].rearrange("q (s t) -> q t s", t=PACK))
-            turned = psum.tile([P, PACK, NQ], F32, name="turned%d" % g, tag="turned", bufs=2)
+            turned = psum.tile([P, PACK, NQ], F32, name="turned%d" % g, tag="turned", bufs=3)
             for t in range(PACK):
-                nc.tensor.transpose(turned[:, t, :], dealt[:, t, :], ident[:])
-            p = keep.tile([P, PACK, NQ], F32, name="p%d" % g, align_bytes=64)
-            for t in range(PACK):
-                nc.scalar.activation(p[:, t, :], turned[:, t, :], ACT.Silu, bias=kb_col[g][:, t : t + 1])
-            silu.append(p)
+                nc.tensor.matmul(turned[:, t, :], dealt[:, t, :], ident[:], is_transpose=True, start=(t == 0), stop=False)
+            sums.append(turned)
 
-        vsc_pool = keep.tile([P, POOL_PAGES * DV], U8, name="vsc_pool", tag="a", align_bytes=64)
-        nc.vector.memset(vsc_pool[:].bitcast(I32), 0)
+        vw_pool = keep.tile([P, POOL_PAGES * DV], U32, name="vw_pool", tag="a", align_bytes=64)
+        nc.sync.dma_start(
+            vw_pool[:].bitcast(I32).rearrange("p (u e) -> p u e", u=POOL_PAGES),
+            v_words.rearrange("u p e r -> p u (e r)").bitcast(I32),
+        )
+
+        vsc_pool = keep.tile([P, POOL_PAGES * DV], U8, name="vsc_pool", tag="c", align_bytes=64)
+        nc.gpsimd.memset(vsc_pool[:].bitcast(I32), 0)
         vsc_rows = v_scales.rearrange("u (a r) e -> r a u e", r=PACK)
         for r in range(PACK):
             nc.sync.dma_start(
@@ -117,38 +112,48 @@ def tile_attend_pkv8_silu_bias_kernel(tc, qT, k_words, k_scales, v_words, v_scal
                 vsc_rows[r].bitcast(I32),
             )
 
-        w_codes, w_scales = [], []
+        silu = []
         for g in range(PAGES):
-            vs_row = keep.tile([P, PAGE], F32, name="vs_row%d" % g, align_bytes=64)
-            nc.vector.tensor_copy(vs_row[:], vs_pool[:].indirect(page_slots(g)))
-            vs_col = to_columns(vs_row, "vs_col%d" % g)
-            w = keep.tile([P, PACK, NQ], BF16, name="w%d" % g, align_bytes=64)
+            kb_row = keep.tile([P, PAGE], F32, name="kb_row%d" % g, align_bytes=64)
+            nc.vector.tensor_copy(kb_row[:], kb_pool[:].indirect(page_slots(g)))
             for t in range(PACK):
-                nc.scalar.activation(w[:, t, :], silu[g][:, t, :], ACT.Copy, scale=vs_col[:, t : t + 1])
-            woven = keep.tile([P, NQ, PACK], BF16, name="woven%d" % g, align_bytes=64)
-            nc.scalar.copy(woven[:], w[:].rearrange("s t q -> s q t"))
-            w_codes.append(keep.tile([P, NQ], U32, name="w_codes%d" % g, align_bytes=64))
-            w_scales.append(keep.tile([P, NQ], U8, name="w_scales%d" % g, align_bytes=64))
-            silu[g] = woven
+                nc.tensor.matmul(
+                    sums[g][:, t, :], kb_row[:, t:PAGE:PACK], ident[:], is_transpose=True, start=False, stop=(t == PACK - 1)
+                )
+            p = keep.tile([P, NQ, PACK], F32, name="p%d" % g, tag="p%d" % g, align_bytes=64)
+            nc.scalar.activation(p[:], sums[g][:].rearrange("s t q -> s q t"), ACT.Silu)
+            silu.append(p)
 
-        vsc = keep.tile([P, PAGES * DV], U8, name="vsc", align_bytes=64)
+        vsc = keep.tile([P, PAGES * DV], U8, name="vsc", tag="d", align_bytes=64)
         nc.vector.tensor_copy(vsc[:], vsc_pool[:].indirect(vcols[:]))
         y = psum.tile([P, DV], F32, name="y", tag="y", bufs=1)
-        for g in range(PAGES):
-            vw = keep.tile([P, DV], U32, name="vw%d" % g, align_bytes=64)
-            nc.vector.tensor_copy(vw[:], vw_pool[:].indirect(vcols[:, g * (DV // 16) : (g + 1) * (DV // 16)]))
-            nc.vector.quantize_mx(
-                w_codes[g][:].bitcast(FP8X4), w_scales[g][:], silu[g][:].rearrange("s q t -> s (q t)")
+        for first, count, w_tag, vw_tag in ((0, PAGES - 1, "c", "p0"), (PAGES - 1, 1, "p1", "c")):
+            w = keep.tile([P, count, NQ, PACK], BF16, name="w%d" % first, tag=w_tag, align_bytes=64)
+            for j in range(count):
+                nc.vector.tensor_tensor(
+                    w[:, j],
+                    silu[first + j][:],
+                    vs_col[first + j][:].unsqueeze(1).broadcast_to([P, NQ, PACK]),
+                    mybir.AluOpType.mult,
+                )
+            vw = keep.tile([P, count * DV], U32, name="vw%d" % first, tag=vw_tag, align_bytes=64)
+            nc.vector.tensor_copy(
+                vw[:], vw_pool[:].indirect(vcols[:, first * (DV // 16) : (first + count) * (DV // 16)])
             )
-            nc.tensor.matmul_mx(
-                y[:],
-                lhsT=w_codes[g][:].bitcast(FP8X4),
-                lhsT_scale=w_scales[g][:],
-                rhs=vw[:].bitcast(FP8X4),
-                rhs_scale=vsc[:, g * DV : (g + 1) * DV],
-                start=(g == 0),
-                stop=(g == PAGES - 1),
-            )
+            w_codes = keep.tile([P, count * NQ], U32, name="w_codes%d" % first, align_bytes=64)
+            w_scales = keep.tile([P, count * NQ], U8, name="w_scales%d" % first, align_bytes=64)
+            nc.vector.quantize_mx(w_codes[:].bitcast(FP8X4), w_scales[:], w[:].rearrange("s g q t -> s (g q t)"))
+            for j in range(count):
+                g = first + j
+                nc.tensor.matmul_mx(
+                    y[:],
+                    lhsT=w_codes[:, j * NQ : (j + 1) * NQ].bitcast(FP8X4),
+                    lhsT_scale=w_scales[:, j * NQ : (j + 1) * NQ],
+                    rhs=vw[:, j * DV : (j + 1) * DV].bitcast(FP8X4),
+                    rhs_scale=vsc[:, g * DV : (g + 1) * DV],
+                    start=(g == 0),
+                    stop=(g == PAGES - 1),
+                )
         result = keep.tile([P, DV], F32, name="result", align_bytes=64)
         nc.scalar.activation(result[:], y[:], ACT.Copy, scale=1.0 / 16.0)
         nc.sync.dma_start(out[0], result[:])

@@ -44,6 +44,8 @@ def tile_attend_pkv8_silu_bias_kernel(tc, qT, k_words, k_scales, v_words, v_scal
         for r in range(PACK):
             nc.sync.dma_start(ks_pool[r:P:32, :].bitcast(I32), ks_rows[r].bitcast(I32))
         nc.sync.dma_start(q_raw[:], qT[0].rearrange("(p j) q -> p j q", j=PACK))
+        kb_rows = keep.tile([P, P], F32, name="kb_rows", align_bytes=64)
+        nc.sync.dma_start(kb_rows[:], kb[0 : P * P // T, :].rearrange("r (j c) -> (r j) c", c=P))
         nc.sync.dma_start(vs_pool[0:1, :], vs[0:1, :])
         nc.sync.dma_start(vcols[:], voffs)
 
@@ -61,8 +63,24 @@ def tile_attend_pkv8_silu_bias_kernel(tc, qT, k_words, k_scales, v_words, v_scal
         q_scales = keep.tile([P, NQ], U8, name="q_scales", align_bytes=64)
         nc.vector.quantize_mx(q_codes[:].bitcast(FP8X4), q_scales[:], q_bf[:].rearrange("p q j -> p (q j)"))
 
-        kb_pool = keep.tile([P, T], F32, name="kb_pool", tag="d", align_bytes=64)
-        nc.sync.dma_start(kb_pool[:], kb)
+        vw_pool = keep.tile([P, POOL_PAGES * DV], U32, name="vw_pool", tag="d", align_bytes=64)
+        nc.sync.dma_start(
+            vw_pool[:].bitcast(I32).rearrange("p (u e) -> p u e", u=POOL_PAGES),
+            v_words.rearrange("u p e r -> p u (e r)").bitcast(I32),
+        )
+
+        kb_pool = keep.tile([P, T], F32, name="kb_pool", tag="k", align_bytes=64)
+        kb_turned = psum.tile([P, P], F32, name="kb_turned", tag="turned", bufs=3)
+        nc.tensor.transpose(kb_turned[:], kb_rows[:], ident[:])
+        kb_cols = keep.tile([P, T // P], F32, name="kb_cols", align_bytes=64)
+        nc.scalar.activation(kb_cols[:], kb_turned[:, : T // P], ACT.Copy)
+        for u in range(POOL_PAGES):
+            spread = psum.tile([P, PACK, P], F32, name="spread%d" % u, tag="turned", bufs=3)
+            for i in range(PACK):
+                j = PACK * u + i
+                nc.tensor.transpose(spread[:, i, :], kb_cols[:, j : j + 1].to_broadcast([P, P]), ident[:])
+            nc.scalar.activation(kb_pool[:, u * PAGE : (u + 1) * PAGE], spread[:].rearrange("p i c -> p (i c)"), ACT.Copy)
+
         vs_row = keep.tile([P, N], F32, name="vs_row", align_bytes=64)
         nc.vector.tensor_copy(vs_row[:], vs_pool[:].indirect(slots[:]))
 
@@ -97,12 +115,6 @@ def tile_attend_pkv8_silu_bias_kernel(tc, qT, k_words, k_scales, v_words, v_scal
                 nc.tensor.matmul(turned[:, t, :], dealt[:, t, :], ident[:], is_transpose=True, start=(t == 0), stop=False)
             sums.append(turned)
 
-        vw_pool = keep.tile([P, POOL_PAGES * DV], U32, name="vw_pool", tag="a", align_bytes=64)
-        nc.sync.dma_start(
-            vw_pool[:].bitcast(I32).rearrange("p (u e) -> p u e", u=POOL_PAGES),
-            v_words.rearrange("u p e r -> p u (e r)").bitcast(I32),
-        )
-
         vsc_pool = keep.tile([P, POOL_PAGES * DV], U8, name="vsc_pool", tag="c", align_bytes=64)
         nc.gpsimd.memset(vsc_pool[:].bitcast(I32), 0)
         vsc_rows = v_scales.rearrange("u (a r) e -> r a u e", r=PACK)
@@ -113,9 +125,10 @@ def tile_attend_pkv8_silu_bias_kernel(tc, qT, k_words, k_scales, v_words, v_scal
             )
 
         silu = []
+        kb_slots = keep.tile([P, N], F32, name="kb_slots", tag="a", align_bytes=64)
         for g in range(PAGES):
-            kb_row = keep.tile([P, PAGE], F32, name="kb_row%d" % g, align_bytes=64)
-            nc.vector.tensor_copy(kb_row[:], kb_pool[:].indirect(page_slots(g)))
+            kb_row = kb_slots[:, g * PAGE : (g + 1) * PAGE]
+            nc.vector.tensor_copy(kb_row, kb_pool[:].indirect(page_slots(g)))
             for t in range(PACK):
                 nc.tensor.matmul(
                     sums[g][:, t, :], kb_row[:, t:PAGE:PACK], ident[:], is_transpose=True, start=False, stop=(t == PACK - 1)
@@ -124,7 +137,7 @@ def tile_attend_pkv8_silu_bias_kernel(tc, qT, k_words, k_scales, v_words, v_scal
             nc.scalar.activation(p[:], sums[g][:].rearrange("s t q -> s q t"), ACT.Silu)
             silu.append(p)
 
-        vsc = keep.tile([P, PAGES * DV], U8, name="vsc", tag="d", align_bytes=64)
+        vsc = keep.tile([P, PAGES * DV], U8, name="vsc", tag="k", align_bytes=64)
         nc.vector.tensor_copy(vsc[:], vsc_pool[:].indirect(vcols[:]))
         y = psum.tile([P, DV], F32, name="y", tag="y", bufs=1)
         for first, count, w_tag, vw_tag in ((0, PAGES - 1, "c", "p0"), (PAGES - 1, 1, "p1", "c")):

from contextlib import ExitStack

import concourse.mybir as mybir
from concourse.masks import make_identity

N, T, D, DV, NQ = 1536, 4096, 512, 256, 128
P = 128
PACK = 4
PAGE = 512
PAGES = N // PAGE
POOL_PAGES = T // PAGE
BYTES = 4 * D * NQ + T * (D + DV) + T * (D + DV) // 32 + 2 * 4 * T + 2 * P * (N + PAGES * DV) // 16 + 4 * NQ * DV
FLOPS = 2 * NQ * N * (D + DV)

F32 = mybir.dt.float32
BF16 = mybir.dt.bfloat16
I32 = mybir.dt.int32
U32 = mybir.dt.uint32
U16 = mybir.dt.uint16
U8 = mybir.dt.uint8
FP8X4 = mybir.dt.float8_e4m3fn_x4
ACT = mybir.ActivationFunctionType


def tile_attend_pkv8_silu_bias_kernel(tc, qT, k_words, k_scales, v_words, v_scales, vs, kb, offs, voffs, out):
    nc = tc.nc
    with ExitStack() as ctx:
        keep = ctx.enter_context(tc.tile_pool(name="keep", bufs=1))
        psum = ctx.enter_context(tc.psum_pool(name="psum", bufs=1))

        slots = keep.tile([P, N // 16], U16, name="slots")
        vcols = keep.tile([P, PAGES * DV // 16], U16, name="vcols")
        ks_pool = keep.tile([P, T], U8, name="ks_pool", tag="b", align_bytes=64)
        vs_pool = keep.tile([P, T], F32, name="vs_pool", tag="c", align_bytes=64)
        q_raw = keep.tile([P, PACK, NQ], F32, name="q_raw", tag="a", align_bytes=64)
        ident = keep.tile([P, P], F32, name="ident", align_bytes=64)

        nc.vector.memset(ks_pool[:].bitcast(I32), 0)
        nc.vector.memset(vs_pool[:].bitcast(I32), 0)
        make_identity(nc, ident[:])

        nc.sync.dma_start(slots[:], offs)
        ks_rows = k_scales[0].rearrange("(a r) c -> r a c", r=PACK)
        for r in range(PACK):
            nc.sync.dma_start(ks_pool[r:P:32, :].bitcast(I32), ks_rows[r].bitcast(I32))
        nc.sync.dma_start(q_raw[:], qT[0].rearrange("(p j) q -> p j q", j=PACK))
        kb_rows = keep.tile([P, P], F32, name="kb_rows", align_bytes=64)
        nc.sync.dma_start(kb_rows[:], kb[0 : P * P // T, :].rearrange("r (j c) -> (r j) c", c=P))
        nc.sync.dma_start(vs_pool[0:1, :], vs[0:1, :])
        nc.sync.dma_start(vcols[:], voffs)

        def page_slots(g):
            return slots[:, g * (PAGE // 16) : (g + 1) * (PAGE // 16)]

        ks = keep.tile([P, N], U8, name="ks", align_bytes=64)
        nc.vector.tensor_copy(ks[:], ks_pool[:].indirect(slots[:]))

        q_bf = keep.tile([P, NQ, PACK], BF16, name="q_bf", tag="d", align_bytes=64)
        nc.scalar.copy(q_bf[:], q_raw[:].rearrange("p j q -> p q j"))
        kw_pool = keep.tile([P, T], U32, name="kw_pool", tag="a", align_bytes=64)
        nc.sync.dma_start(kw_pool[:].bitcast(I32), k_words[0].rearrange("p n r -> p (n r)").bitcast(I32))
        q_codes = keep.tile([P, NQ], U32, name="q_codes", tag="b", align_bytes=64)
        q_scales = keep.tile([P, NQ], U8, name="q_scales", align_bytes=64)
        nc.vector.quantize_mx(q_codes[:].bitcast(FP8X4), q_scales[:], q_bf[:].rearrange("p q j -> p (q j)"))

        vw_pool = keep.tile([P, POOL_PAGES * DV], U32, name="vw_pool", tag="d", align_bytes=64)
        nc.sync.dma_start(
            vw_pool[:].bitcast(I32).rearrange("p (u e) -> p u e", u=POOL_PAGES),
            v_words.rearrange("u p e r -> p u (e r)").bitcast(I32),
        )

        kb_pool = keep.tile([P, T], F32, name="kb_pool", tag="k", align_bytes=64)
        kb_turned = psum.tile([P, P], F32, name="kb_turned", tag="turned", bufs=3)
        nc.tensor.transpose(kb_turned[:], kb_rows[:], ident[:])
        kb_cols = keep.tile([P, T // P], F32, name="kb_cols", align_bytes=64)
        nc.scalar.activation(kb_cols[:], kb_turned[:, : T // P], ACT.Copy)
        for u in range(POOL_PAGES):
            spread = psum.tile([P, PACK, P], F32, name="spread%d" % u, tag="turned", bufs=3)
            for i in range(PACK):
                j = PACK * u + i
                nc.tensor.transpose(spread[:, i, :], kb_cols[:, j : j + 1].to_broadcast([P, P]), ident[:])
            nc.scalar.activation(kb_pool[:, u * PAGE : (u + 1) * PAGE], spread[:].rearrange("p i c -> p (i c)"), ACT.Copy)

        vs_row = keep.tile([P, N], F32, name="vs_row", align_bytes=64)
        nc.vector.tensor_copy(vs_row[:], vs_pool[:].indirect(slots[:]))

        def to_columns(row, name):
            bank = psum.tile([P, PACK, P], F32, name=name + "_bank", tag="turn", bufs=2)
            for t in range(PACK):
                nc.tensor.transpose(bank[:, t, :], row[:, t:PAGE:PACK], ident[:])
            col = keep.tile([P, PACK], F32, name=name)
            nc.scalar.copy(col[:], bank[:, :, 0])
            return col

        vs_col = [to_columns(vs_row[:, g * PAGE : (g + 1) * PAGE], "vs_col%d" % g) for g in range(PAGES)]

        sums = []
        for g in range(PAGES):
            kw = keep.tile([P, PAGE], U32, name="kw%d" % g, align_bytes=64)
            nc.vector.tensor_copy(kw[:], kw_pool[:].indirect(page_slots(g)))
            score = psum.tile([P, PAGE], F32, name="score%d" % g, tag="score", bufs=2)
            nc.tensor.matmul_mx(
                score[:],
                lhsT=q_codes[:].bitcast(FP8X4),
                lhsT_scale=q_scales[:],
                rhs=kw[:].bitcast(FP8X4),
                rhs_scale=ks[:, g * PAGE : (g + 1) * PAGE],
                start=True,
                stop=True,
            )
            dealt = keep.tile([P, PACK, P], F32, name="dealt%d" % g, align_bytes=64)
            nc.scalar.copy(dealt[:], score[:].rearrange("q (s t) -> q t s", t=PACK))
            turned = psum.tile([P, PACK, NQ], F32, name="turned%d" % g, tag="turned", bufs=3)
            for t in range(PACK):
                nc.tensor.matmul(turned[:, t, :], dealt[:, t, :], ident[:], is_transpose=True, start=(t == 0), stop=False)
            sums.append(turned)

        vsc_pool = keep.tile([P, POOL_PAGES * DV], U8, name="vsc_pool", tag="c", align_bytes=64)
        nc.gpsimd.memset(vsc_pool[:].bitcast(I32), 0)
        vsc_rows = v_scales.rearrange("u (a r) e -> r a u e", r=PACK)
        for r in range(PACK):
            nc.sync.dma_start(
                vsc_pool[r:P:32, :].bitcast(I32).rearrange("a (u e) -> a u e", u=POOL_PAGES),
                vsc_rows[r].bitcast(I32),
            )

        silu = []
        kb_slots = keep.tile([P, N], F32, name="kb_slots", tag="a", align_bytes=64)
        for g in range(PAGES):
            kb_row = kb_slots[:, g * PAGE : (g + 1) * PAGE]
            nc.vector.tensor_copy(kb_row, kb_pool[:].indirect(page_slots(g)))
            for t in range(PACK):
                nc.tensor.matmul(
                    sums[g][:, t, :], kb_row[:, t:PAGE:PACK], ident[:], is_transpose=True, start=False, stop=(t == PACK - 1)
                )
            p = keep.tile([P, NQ, PACK], F32, name="p%d" % g, tag="p%d" % g, align_bytes=64)
            nc.scalar.activation(p[:], sums[g][:].rearrange("s t q -> s q t"), ACT.Silu)
            silu.append(p)

        vsc = keep.tile([P, PAGES * DV], U8, name="vsc", tag="k", align_bytes=64)
        nc.vector.tensor_copy(vsc[:], vsc_pool[:].indirect(vcols[:]))
        y = psum.tile([P, DV], F32, name="y", tag="y", bufs=1)
        for first, count, w_tag, vw_tag in ((0, PAGES - 1, "c", "p0"), (PAGES - 1, 1, "p1", "c")):
            w = keep.tile([P, count, NQ, PACK], BF16, name="w%d" % first, tag=w_tag, align_bytes=64)
            for j in range(count):
                nc.vector.tensor_tensor(
                    w[:, j],
                    silu[first + j][:],
                    vs_col[first + j][:].unsqueeze(1).broadcast_to([P, NQ, PACK]),
                    mybir.AluOpType.mult,
                )
            vw = keep.tile([P, count * DV], U32, name="vw%d" % first, tag=vw_tag, align_bytes=64)
            nc.vector.tensor_copy(
                vw[:], vw_pool[:].indirect(vcols[:, first * (DV // 16) : (first + count) * (DV // 16)])
            )
            w_codes = keep.tile([P, count * NQ], U32, name="w_codes%d" % first, align_bytes=64)
            w_scales = keep.tile([P, count * NQ], U8, name="w_scales%d" % first, align_bytes=64)
            nc.vector.quantize_mx(w_codes[:].bitcast(FP8X4), w_scales[:], w[:].rearrange("s g q t -> s (g q t)"))
            for j in range(count):
                g = first + j
                nc.tensor.matmul_mx(
                    y[:],
                    lhsT=w_codes[:, j * NQ : (j + 1) * NQ].bitcast(FP8X4),
                    lhsT_scale=w_scales[:, j * NQ : (j + 1) * NQ],
                    rhs=vw[:, j * DV : (j + 1) * DV].bitcast(FP8X4),
                    rhs_scale=vsc[:, g * DV : (g + 1) * DV],
                    start=(g == 0),
                    stop=(g == PAGES - 1),
                )
        result = keep.tile([P, DV], F32, name="result", align_bytes=64)
        nc.scalar.activation(result[:], y[:], ACT.Copy, scale=1.0 / 16.0)
        nc.sync.dma_start(out[0], result[:])
